import numpy as np
CORES = [5,29,101,125,133,157,229,253]
N = 8
T, SQ = 2048, 1024
def entries(a): return a.T.reshape(-1)
def pack(v, P): return np.ascontiguousarray(np.asarray(v, np.int32).reshape(-1, P).T)
def lists(rng, how):
    h = N // 2; d = rng.integers(0, SQ, h); n = np.full(N, SQ); p = rng.permutation(N); n[p[0:2 * h:2]] += d; n[p[1:2 * h:2]] -= d
    if how == "back": g = int(rng.integers(2, h + 1)); n[:] = 0; n[N - g:] = T
    if how == "ends": d = rng.integers(SQ // 4, SQ - 1, h); n[:] = SQ; n[:h] += d; n[N - h:] -= d
    if how == "front": n[:] = 0; n[:h] = T; n[h] = (N - 2 * h) * SQ
    if how == "late": n[:] = 0; n[int(rng.integers(N - 1))] = int(rng.integers(1, SQ)); n[N - 1] = T
    if how == "tail": g = min(3, N // 3); n = rng.integers(SQ // 8, SQ // 4, N); n[N - g:] = T - n[N - g:]
    F = np.zeros((N, T), np.int64)
    for r in range(N):
        o = rng.permutation(T)
        if how == "ends": o = np.concatenate([[0, T - 1], 1 + rng.permutation(T - 2)])
        F[r, o[:n[r]]] = 1
    return {"fl": np.stack([pack(f, 16) for f in F])}
def setup_inputs(rng):
    return dict({"x": rng.standard_normal((N, 128, T), dtype=np.float32), "st": rng.standard_normal((N, 128, SQ), dtype=np.float32)}, **lists(rng, "uniform"))
def setup_inputs_back(rng):
    d = setup_inputs(rng); d.update(lists(rng, "back"))
    for k in ("x", "st"): d[k] = (d[k].astype(np.float32) * 1048576.0).astype(d[k].dtype)
    return d
def setup_inputs_ends(rng):
    d = setup_inputs(rng); d.update(lists(rng, "ends"))
    for k in ("x", "st"): d[k] = (d[k].astype(np.float32) * (1 / 1024.0)).astype(d[k].dtype)
    return d
def setup_inputs_front(rng):
    d = setup_inputs(rng); d.update(lists(rng, "front"))
    return d
def setup_inputs_late(rng):
    d = setup_inputs(rng); d.update(lists(rng, "late"))
    return d
def setup_inputs_tail(rng):
    d = setup_inputs(rng); d.update(lists(rng, "tail"))
    return d
def check_inputs(x):
    bad = []
    if x["fl"].min() < 0 or x["fl"].max() >= 2: bad.append("fl out of range")
    if int(x["fl"].sum()) > N * SQ: bad.append("more flags than the stream has columns")
    return bad
def reference(x, st, fl):
    S = np.concatenate(list(st), axis=1); X = np.concatenate(list(x), axis=1)
    F = np.concatenate([entries(f) for f in fl]) > 0; c = np.cumsum(F) - F
    Y = np.where(F[None, :], S[:, np.minimum(c, N * SQ - 1)], X)
    return {"y": np.stack([Y[:, T * r:T * r + T] for r in range(N)])}

@@ -1,0 +1,314 @@
+from concourse.bass import DstId, RemoteDMATransfer
+from concourse.mybir import AluOpType as A, AxisListType, ActivationFunctionType as Act
+
+N = 8
+TC = 2048
+SQ = 1024
+M = 8
+B = SQ // M
+NCORES = 256
+
+SCRATCH = {
+    "fland": ("dram", [N, 128, 16], "int32"),
+    "fall": ("sbuf", [128, 128], "int32"),
+    "fallf": ("sbuf", [128, 128], "float32"),
+    "rsum": ("sbuf", [128, 8], "float32"),
+    "pint": ("sbuf", [128, 128], "int32"),
+    "cint": ("sbuf", [128, 128], "int32"),
+    "p15": ("sbuf", [128, 128], "int32"),
+    "sint": ("sbuf", [128, 128], "int32"),
+    "vc": ("sbuf", [128, 128], "float32"),
+    "onef": ("sbuf", [128, 128], "float32"),
+    "maskf": ("sbuf", [128, 128], "float32"),
+    "i1": ("sbuf", [128, 128], "int32"),
+    "i2": ("sbuf", [128, 128], "int32"),
+    "i3": ("sbuf", [128, 128], "int32"),
+    "off": ("sbuf", [128, 128], "uint16"),
+    "ps1": ("psum", [128, 512], "float32"),
+    "ps2": ("psum", [128, 512], "float32"),
+    "ps3": ("psum", [128, 512], "float32"),
+    "ps4": ("psum", [128, 512], "float32"),
+    "oneb": ("sbuf", [128, 128], "bfloat16"),
+    "me": ("sbuf", [128, 64], "bfloat16"),
+    "part": ("sbuf", [128, 4 * B], "float32"),
+    "pick": ("sbuf", [128, N * B], "float32"),
+    "f16": ("sbuf", [16, 128], "int32"),
+    "fb": ("sbuf", [16, 128], "bfloat16"),
+    "zb": ("sbuf", [16, 128], "bfloat16"),
+    "leq": ("sbuf", [16, 128], "bfloat16"),
+    "lpre": ("sbuf", [16, 128], "bfloat16"),
+    "zero": ("sbuf", [128, 128], "float32"),
+    "cum": ("sbuf", [128, 128], "float32"),
+    "t1": ("sbuf", [128, 128], "float32"),
+    "nf": ("sbuf", [128, 128], "float32"),
+    "fr": ("sbuf", [128, 128], "float32"),
+    "xc": ("sbuf", [128, 128], "float32"),
+    "stt": ("sbuf", [128, SQ], "float32"),
+    "win": ("sbuf", [128, 2 * TC], "float32"),
+    "yt": ("sbuf", [128, TC], "float32"),
+}
+SEMAPHORES = ["s_fl", "s_f16", "s_st0", "s_st1", "s_x", "s_y", "s_fall", "s_fa", "s_fb", "s_d", "s_r",
+              "l_fl", "l_d", "l_rel", "l_s", "vs", "gs", "ts", "yv", "ys", "pv", "pa"]
+
+_CACHE = {}
+
+
+def _layout(topo, cores):
+    if "lay" in _CACHE:
+        return _CACHE["lay"]
+    first = [r for r in range(N) if r == 0 or topo.same_plane(cores[0], cores[r])]
+    planes = [first, [r for r in range(N) if r not in first]]
+    for e in range(2):
+        if planes[e] != list(range(e, N, 2)):
+            raise ValueError("the design needs the stream's even parts in one plane, the odd ones in the other")
+    owners = [c for c in range(NCORES) if c not in cores and all(topo.may_write(c, r) for r in cores)]
+    helpers = [[], []]
+    for e in range(2):
+        for r in planes[e]:
+            k = cores[r]
+            helpers[e].append([c for c in owners if topo.host(c) == topo.host(k) and topo.chip(c) == topo.chip(k)
+                               and topo.die(c) == topo.die(k)][0])
+    for e in range(2):
+        for r in planes[1 - e]:
+            k = cores[r]
+            helpers[e].append([c for c in owners if topo.mates(c, k) and topo.die(c) != topo.die(k)][0])
+    _CACHE["lay"] = (planes, helpers)
+    return _CACHE["lay"]
+
+
+def _dst(topo, dst, src):
+    rid, pid = topo.addr(dst, src)
+    return DstId(rid=rid, pnc=pid)
+
+
+def _engines(topo, src, dsts):
+    m = topo.mask(src, dsts[0])
+    for d in dsts[1:]:
+        m &= topo.mask(src, d)
+    out, b = [], 1
+    while b <= m:
+        if m & b:
+            out.append(b)
+        b *= 2
+    return out
+
+
+class _Chain:
+    pass
+
+
+def _step(q, sem, n):
+    def do(ins):
+        ins.then_inc(sem, 1)
+        n[0] += 1
+        return n[0]
+
+    def wait():
+        q.wait_ge(sem, n[0])
+    return do, wait
+
+
+def rank_program(g, core, T, topo):
+    cores = list(T.cores)
+    planes, helpers = _layout(topo, cores)
+    rank = T.rank_of(core)
+    if rank is not None:
+        _rank(g, core, T, topo, cores, planes, helpers, rank)
+        return
+    for e in range(2):
+        if core in helpers[e]:
+            _helper(g, core, T, topo, cores, planes, helpers, e, helpers[e].index(core))
+
+
+def _rank(g, core, T, topo, cores, planes, helpers, rank):
+    S = T.sem
+    e = rank % 2
+    q = planes[e].index(rank)
+    V, P, C = g.vector, g.tensor, g.scalar
+
+    g.sync.dma_start(T.fland[rank], T.fl[:]).then_inc(S.s_fl, 16)
+    H = SQ // 2
+    C.dma_start(T.stt[:, 0:H], T.st[:, 0:H]).then_inc(S.s_st0, 16)
+    C.dma_start(T.stt[:, H:SQ], T.st[:, H:SQ]).then_inc(S.s_st1, 16)
+    g.sync.dma_start(T.f16[:], T.fl[:]).then_inc(S.s_f16, 16)
+
+    dsts = helpers[e] + [cores[r] for r in planes[e] if r != rank]
+    eng = _engines(topo, core, dsts)
+    g.wait_ge(S.s_fl, 16)
+    g.remote_dma_fused([RemoteDMATransfer(
+        dst_ids=[_dst(topo, d, core) for d in dsts], dma_engine_mask=sum(eng), remote_sem=S.s_fa,
+        srcs=[T.fland[rank]], dsts=[T.fland[rank] for d in dsts])], local_sem=S.l_fl)
+    half = M // 2
+    per = len(eng) // half
+    for h in range(2):
+        g.wait_ge(S.s_st0 if h == 0 else S.s_st1, 16)
+        tr = []
+        for k in range(half):
+            i = h * half + k
+            tr.append(RemoteDMATransfer(
+                dst_ids=[_dst(topo, helpers[e][i], core)], dma_engine_mask=sum(eng[k * per:(k + 1) * per]),
+                remote_sem=S.s_d, srcs=[T.stt[:, i * B:(i + 1) * B]], dsts=[T.part[:, q * B:(q + 1) * B]]))
+        g.remote_dma_fused(tr, local_sem=S.l_d)
+
+    vn, gn, tn = [0], [0], [0]
+    vdo, vwait = _step(V, S.vs, vn)
+    gdo, gwait = _step(g, S.gs, gn)
+    tdo, twait = _step(P, S.ts, tn)
+    vdo(V.memset(T.oneb[0:16, :], 1.0))
+    vdo(V.memset(T.zb[:], 0.0))
+    vdo(V.memset(T.zero[:], 0.0))
+    n_mem = vdo(V.memset(T.onef[:], 1.0))
+    g.wait_ge(S.vs, n_mem)
+    gdo(g.affine_select(T.lpre[:], T.zb[:], [[0, 8], [1, 16]], A.is_gt, -1.0, 0, -1))
+    n_lhs = gdo(g.affine_select(T.leq[:], T.oneb[0:16, :], [[0, 8], [1, 16]], A.is_equal, 0.0, 0, -1))
+    gdo(g.iota(T.pint[:], [[0, 128]], 0, 1))
+    n_iota = gdo(g.iota(T.cint[:], [[16, 128]], TC, 0))
+    n_mask = gdo(g.affine_select(T.maskf[:], T.onef[:], [[0, 128]], A.is_gt, 0.0, 16 * rank, -1))
+
+    V.wait_ge(S.s_f16, 16)
+    n_fb = vdo(V.tensor_copy(T.fb[:], T.f16[:]))
+    P.wait_ge(S.vs, n_fb)
+    n_a = tdo(P.matmul(T.ps1[:, 0:128], T.oneb[0:16, :], T.fb[:], True, True))
+    P.wait_ge(S.gs, n_lhs)
+    tdo(P.matmul(T.ps2[:, 0:128], T.lpre[:], T.fb[:], True, True))
+    n_e = tdo(P.matmul(T.ps3[:, 0:128], T.leq[:], T.fb[:], True, True))
+    V.wait_ge(S.ts, n_a)
+    V.wait_ge(S.vs, n_fb)
+    vdo(V.tensor_tensor_scan(T.cum[:], T.ps1[:, 0:128], T.zero[:], 0.0, A.add, A.add))
+    V.wait_ge(S.ts, n_e)
+    vwait()
+    vdo(V.tensor_tensor(T.t1[:], T.cum[:], T.ps2[:, 0:128], A.add))
+    vdo(V.tensor_copy(T.fr[:], T.ps3[:, 0:128]))
+    vdo(V.tensor_scalar(T.nf[:], T.ps3[:, 0:128], -1.0, 1.0, A.mult, A.add))
+    V.wait_ge(S.gs, n_iota)
+    vdo(V.tensor_scalar(T.p15[:], T.pint[:], 15, None, A.bitwise_and))
+    vwait()
+    vdo(V.tensor_tensor(T.vc[:], T.p15[:], T.cint[:], A.add))
+    vwait()
+    vdo(V.tensor_tensor(T.xc[:], T.vc[:], T.nf[:], A.mult))
+
+    g.sync.wait_ge(S.s_fl, 16)
+    g.sync.wait_ge(S.s_fa, 3 * len(eng))
+    g.sync.wait_ge(S.s_fb, len(eng))
+    g.sync.dma_start(T.fall[:], T.fland[:]).then_inc(S.s_fall, 16)
+    V.wait_ge(S.s_fall, 16)
+    vdo(V.tensor_copy(T.fallf[:], T.fall[:]))
+    vwait()
+    n_rs = vdo(V.tensor_reduce(T.rsum[:, 0:1], T.fallf[:], AxisListType.X, A.add))
+    P.wait_ge(S.gs, n_mask)
+    P.wait_ge(S.vs, n_rs)
+    n_c = tdo(P.matmul(T.ps4[:, 0:1], T.maskf[:], T.rsum[:, 0:1], True, True))
+    V.wait_ge(S.ts, n_c)
+    vwait()
+    vdo(V.tensor_scalar(T.i1[:], T.t1[:], T.ps4[:, 0:1], None, A.add))
+    vwait()
+    vdo(V.tensor_scalar(T.i2[:], T.i1[:], TC - 1, None, A.bitwise_and))
+    vwait()
+    vdo(V.tensor_tensor(T.i3[:], T.i2[:], T.fr[:], A.mult))
+    vwait()
+    vdo(V.tensor_tensor(T.i1[:], T.i3[:], T.xc[:], A.add))
+    vwait()
+    n_off = vdo(V.tensor_copy(T.off[:], T.i1[:]))
+
+    C.wait_ge(S.l_d, 2 * len(eng))
+    C.dma_start(T.win[:, TC:2 * TC], T.x[:]).then_inc(S.s_x, 16)
+
+    W = TC // 4
+    for qu in (V, C):
+        qu.wait_ge(S.vs, n_off)
+        qu.wait_ge(S.s_x, 16)
+        qu.wait_ge(S.s_r, 2 * M)
+    for k in range(2):
+        a = k * W
+        V.tensor_copy(T.yt[:, a:a + W], T.win[:].indirect(T.off[:, a // 16:(a + W) // 16])).then_inc(S.yv, 1)
+        b = (k + 2) * W
+        C.activation(T.yt[:, b:b + W], T.win[:].indirect(T.off[:, b // 16:(b + W) // 16]), Act.Copy).then_inc(S.ys, 1)
+    for k in range(2):
+        for sem, o in ((S.yv, 0), (S.ys, 2)):
+            a = (k + o) * W
+            g.sync.wait_ge(sem, k + 1)
+            g.sync.dma_start(T.y[:, a:a + W], T.yt[:, a:a + W]).then_inc(S.s_y, 16)
+    g.sync.wait_ge(S.s_y, 64)
+    g.wait_ge(S.l_fl, len(eng))
+    g.wait_ge(S.l_d, 2 * len(eng))
+    g.wait_ge(S.gs, gn[0])
+
+
+def _helper(g, core, T, topo, cores, planes, helpers, e, i):
+    S = T.sem
+    V, P, C = g.vector, g.tensor, g.scalar
+    base = e * SQ + i * B
+    n = N * B // 16
+    w = B // 16
+    vn, gn, tn = [0], [0], [0]
+    vdo, vwait = _step(V, S.vs, vn)
+    gdo, gwait = _step(g, S.gs, gn)
+    tdo, twait = _step(P, S.ts, tn)
+
+    n_mem = vdo(V.memset(T.onef[:, 0:n], 1.0))
+    vdo(V.memset(T.oneb[:], 1.0))
+    gdo(g.iota(T.pint[:, 0:n], [[0, n]], 0, 1))
+    n_iota = gdo(g.iota(T.cint[:, 0:n], [[0, N], [16, w]], 0, 0))
+    g.wait_ge(S.vs, n_mem)
+    n_mask = gdo(g.affine_select(T.maskf[:, 0:n], T.onef[:, 0:n], [[16, N], [0, w]], A.is_gt, 0.0, 0, -1))
+    V.wait_ge(S.gs, n_iota)
+    vdo(V.tensor_scalar(T.p15[:, 0:n], T.pint[:, 0:n], 15, None, A.bitwise_and))
+    vwait()
+    vdo(V.tensor_tensor(T.sint[:, 0:n], T.p15[:, 0:n], T.cint[:, 0:n], A.add))
+    vwait()
+    vdo(V.tensor_scalar(T.vc[:, 0:n], T.sint[:, 0:n], -1.0, float(TC - 1 - base), A.mult, A.add))
+
+    dsts = [c for c in helpers[1 - e] if topo.mates(c, core)] + [c for c in cores if topo.mates(c, core)]
+    eng = _engines(topo, core, dsts)
+    per = len(eng) // len(planes[e])
+    g.wait_ge(S.s_fa, 4 * len(eng))
+    tr = []
+    for k, r in enumerate(planes[e]):
+        tr.append(RemoteDMATransfer(
+            dst_ids=[_dst(topo, d, core) for d in dsts], dma_engine_mask=sum(eng[k * per:(k + 1) * per]),
+            remote_sem=S.s_fb, srcs=[T.fland[r]], dsts=[T.fland[r] for d in dsts]))
+    g.remote_dma_fused(tr, local_sem=S.l_rel)
+
+    g.sync.wait_ge(S.s_fa, 4 * len(eng))
+    g.sync.wait_ge(S.s_fb, len(eng))
+    g.sync.dma_start(T.fall[:], T.fland[:]).then_inc(S.s_fall, 16)
+    V.wait_ge(S.s_fall, 16)
+    vdo(V.tensor_copy(T.fallf[:], T.fall[:]))
+    vwait()
+    vdo(V.tensor_reduce(T.rsum[:, 0:1], T.fallf[:], AxisListType.X, A.add))
+    vwait()
+    V.wait_ge(S.gs, n_mask)
+    n_me = vdo(V.tensor_scalar(T.me[:, 0:n], T.maskf[:, 0:n], T.rsum[:, 0:1], None, A.mult))
+    P.wait_ge(S.vs, n_me)
+    n_c = tdo(P.matmul(T.ps1[:, 0:n], T.oneb[:], T.me[:, 0:n], True, True))
+    V.wait_ge(S.ts, n_c)
+    vwait()
+    vdo(V.tensor_tensor(T.i1[:, 0:n], T.ps1[:, 0:n], T.vc[:, 0:n], A.add))
+    vwait()
+    sh = (TC // B).bit_length() - 1
+    vdo(V.tensor_scalar(T.i2[:, 0:n], T.i1[:, 0:n], sh, 3 * B, A.arith_shift_right, A.bitwise_and))
+    vwait()
+    vdo(V.tensor_tensor(T.i3[:, 0:n], T.i2[:, 0:n], T.sint[:, 0:n], A.add))
+    vwait()
+    n_off = vdo(V.tensor_copy(T.off[:, 0:n], T.i3[:, 0:n]))
+
+    W = N * B // 2
+    for qu in (V, C):
+        qu.wait_ge(S.vs, n_off)
+        qu.wait_ge(S.s_d, 4 * (len(eng) * 2 // M))
+    V.tensor_copy(T.pick[:, 0:W], T.part[:].indirect(T.off[:, 0:W // 16])).then_inc(S.pv, 1)
+    C.activation(T.pick[:, W:2 * W], T.part[:].indirect(T.off[:, W // 16:n]), Act.Copy).then_inc(S.pa, 1)
+
+    eng2 = _engines(topo, core, cores)
+    per = len(eng2) // N
+    g.wait_ge(S.pv, 1)
+    g.wait_ge(S.pa, 1)
+    tr = []
+    for r in range(N):
+        tr.append(RemoteDMATransfer(
+            dst_ids=[_dst(topo, cores[r], core)], dma_engine_mask=sum(eng2[r * per:(r + 1) * per]), remote_sem=S.s_r,
+            srcs=[T.pick[:, r * B:(r + 1) * B]], dsts=[T.win[:, base:base + B]]))
+    g.remote_dma_fused(tr, local_sem=S.l_s)
+    g.wait_ge(S.l_rel, len(eng))
+    g.wait_ge(S.l_s, len(eng2))
+    g.wait_ge(S.gs, gn[0])

@@ -2,6 +2,7 @@ from concourse.bass import DstId, RemoteDMATransfer
 from concourse.mybir import AluOpType as A, AxisListType, ActivationFunctionType as Act
 
 N = 8
+NP = N // 2
 TC = 2048
 SQ = 1024
 M = 8
@@ -9,9 +10,12 @@ B = SQ // M
 NCORES = 256
 
 SCRATCH = {
-    "fland": ("dram", [N, 128, 16], "int32"),
-    "fall": ("sbuf", [128, 128], "int32"),
-    "fallf": ("sbuf", [128, 128], "float32"),
+    "fown": ("dram", [NP, 128, 16], "int32"),
+    "foth": ("dram", [NP, 128, 16], "int32"),
+    "ofl": ("sbuf", [128, 64], "int32"),
+    "tfl": ("sbuf", [128, 64], "int32"),
+    "oflf": ("sbuf", [128, 64], "float32"),
+    "tflf": ("sbuf", [128, 64], "float32"),
     "rsum": ("sbuf", [128, 8], "float32"),
     "pint": ("sbuf", [128, 128], "int32"),
     "cint": ("sbuf", [128, 128], "int32"),
@@ -20,6 +24,7 @@ SCRATCH = {
     "vc": ("sbuf", [128, 128], "float32"),
     "onef": ("sbuf", [128, 128], "float32"),
     "maskf": ("sbuf", [128, 128], "float32"),
+    "maskt": ("sbuf", [128, 128], "float32"),
     "i1": ("sbuf", [128, 128], "int32"),
     "i2": ("sbuf", [128, 128], "int32"),
     "i3": ("sbuf", [128, 128], "int32"),
@@ -30,7 +35,10 @@ SCRATCH = {
     "ps4": ("psum", [128, 512], "float32"),
     "oneb": ("sbuf", [128, 128], "bfloat16"),
     "me": ("sbuf", [128, 64], "bfloat16"),
-    "part": ("sbuf", [128, 4 * B], "float32"),
+    "tfb": ("sbuf", [128, 64], "bfloat16"),
+    "cs": ("sbuf", [64, 128], "bfloat16"),
+    "mt": ("sbuf", [64, 64], "bfloat16"),
+    "part": ("sbuf", [128, NP * B], "float32"),
     "pick": ("sbuf", [128, N * B], "float32"),
     "f16": ("sbuf", [16, 128], "int32"),
     "fb": ("sbuf", [16, 128], "bfloat16"),
@@ -47,8 +55,8 @@ SCRATCH = {
     "win": ("sbuf", [128, 2 * TC], "float32"),
     "yt": ("sbuf", [128, TC], "float32"),
 }
-SEMAPHORES = ["s_fl", "s_f16", "s_st0", "s_st1", "s_x", "s_y", "s_fall", "s_fa", "s_fb", "s_d", "s_r",
-              "l_fl", "l_d", "l_rel", "l_s", "vs", "gs", "ts", "yv", "ys", "pv", "pa"]
+SEMAPHORES = ["s_fl", "s_f16", "s_st0", "s_st1", "s_x", "s_y", "s_fall", "s_oth", "s_fa", "s_fb", "s_d", "s_r",
+              "l_fl", "l_fr", "l_d", "l_rel", "l_rr", "l_s", "vs", "gs", "ts", "yv", "ys", "pv", "pa"]
 
 _CACHE = {}
 
@@ -93,10 +101,6 @@ def _engines(topo, src, dsts):
     return out
 
 
-class _Chain:
-    pass
-
-
 def _step(q, sem, n):
     def do(ins):
         ins.then_inc(sem, 1)
@@ -126,18 +130,21 @@ def _rank(g, core, T, topo, cores, planes, helpers, rank):
     q = planes[e].index(rank)
     V, P, C = g.vector, g.tensor, g.scalar
 
-    g.sync.dma_start(T.fland[rank], T.fl[:]).then_inc(S.s_fl, 16)
+    g.sync.dma_start(T.fown[q], T.fl[:]).then_inc(S.s_fl, 16)
     H = SQ // 2
     C.dma_start(T.stt[:, 0:H], T.st[:, 0:H]).then_inc(S.s_st0, 16)
     C.dma_start(T.stt[:, H:SQ], T.st[:, H:SQ]).then_inc(S.s_st1, 16)
     g.sync.dma_start(T.f16[:], T.fl[:]).then_inc(S.s_f16, 16)
 
-    dsts = helpers[e] + [cores[r] for r in planes[e] if r != rank]
-    eng = _engines(topo, core, dsts)
+    peers = [cores[r] for r in planes[e] if r != rank]
+    eng = _engines(topo, core, helpers[e] + peers)
+
+    def flags(dsts, lsem):
+        g.remote_dma_fused([RemoteDMATransfer(
+            dst_ids=[_dst(topo, d, core) for d in dsts], dma_engine_mask=sum(eng), remote_sem=S.s_fa,
+            srcs=[T.fown[q]], dsts=[T.fown[q] for d in dsts])], local_sem=lsem)
     g.wait_ge(S.s_fl, 16)
-    g.remote_dma_fused([RemoteDMATransfer(
-        dst_ids=[_dst(topo, d, core) for d in dsts], dma_engine_mask=sum(eng), remote_sem=S.s_fa,
-        srcs=[T.fland[rank]], dsts=[T.fland[rank] for d in dsts])], local_sem=S.l_fl)
+    flags(helpers[e], S.l_fl)
     half = M // 2
     per = len(eng) // half
     for h in range(2):
@@ -149,6 +156,8 @@ def _rank(g, core, T, topo, cores, planes, helpers, rank):
                 dst_ids=[_dst(topo, helpers[e][i], core)], dma_engine_mask=sum(eng[k * per:(k + 1) * per]),
                 remote_sem=S.s_d, srcs=[T.stt[:, i * B:(i + 1) * B]], dsts=[T.part[:, q * B:(q + 1) * B]]))
         g.remote_dma_fused(tr, local_sem=S.l_d)
+        if h == 0:
+            flags(peers, S.l_fr)
 
     vn, gn, tn = [0], [0], [0]
     vdo, vwait = _step(V, S.vs, vn)
@@ -163,7 +172,8 @@ def _rank(g, core, T, topo, cores, planes, helpers, rank):
     n_lhs = gdo(g.affine_select(T.leq[:], T.oneb[0:16, :], [[0, 8], [1, 16]], A.is_equal, 0.0, 0, -1))
     gdo(g.iota(T.pint[:], [[0, 128]], 0, 1))
     n_iota = gdo(g.iota(T.cint[:], [[16, 128]], TC, 0))
-    n_mask = gdo(g.affine_select(T.maskf[:], T.onef[:], [[0, 128]], A.is_gt, 0.0, 16 * rank, -1))
+    gdo(g.affine_select(T.maskf[:], T.onef[:], [[0, 128]], A.is_gt, 0.0, 32 * q, -1))
+    n_mask = gdo(g.affine_select(T.maskt[:], T.onef[:], [[0, 128]], A.is_gt, 0.0, 32 * (q + e), -1))
 
     V.wait_ge(S.s_f16, 16)
     n_fb = vdo(V.tensor_copy(T.fb[:], T.f16[:]))
@@ -187,17 +197,22 @@ def _rank(g, core, T, topo, cores, planes, helpers, rank):
     vwait()
     vdo(V.tensor_tensor(T.xc[:], T.vc[:], T.nf[:], A.mult))
 
-    g.sync.wait_ge(S.s_fl, 16)
-    g.sync.wait_ge(S.s_fa, 3 * len(eng))
     g.sync.wait_ge(S.s_fb, len(eng))
-    g.sync.dma_start(T.fall[:], T.fland[:]).then_inc(S.s_fall, 16)
+    g.sync.dma_start(T.tfl[:], T.foth[:]).then_inc(S.s_oth, 16)
+    g.sync.wait_ge(S.s_fl, 16)
+    g.sync.wait_ge(S.s_fa, (NP - 1) * len(eng))
+    g.sync.dma_start(T.ofl[:], T.fown[:]).then_inc(S.s_fall, 16)
+    V.wait_ge(S.s_oth, 16)
+    vdo(V.tensor_copy(T.tflf[:], T.tfl[:]))
     V.wait_ge(S.s_fall, 16)
-    vdo(V.tensor_copy(T.fallf[:], T.fall[:]))
+    vdo(V.tensor_copy(T.oflf[:], T.ofl[:]))
     vwait()
-    n_rs = vdo(V.tensor_reduce(T.rsum[:, 0:1], T.fallf[:], AxisListType.X, A.add))
+    vdo(V.tensor_reduce(T.rsum[:, 1:2], T.tflf[:], AxisListType.X, A.add))
+    n_rs = vdo(V.tensor_reduce(T.rsum[:, 0:1], T.oflf[:], AxisListType.X, A.add))
     P.wait_ge(S.gs, n_mask)
     P.wait_ge(S.vs, n_rs)
-    n_c = tdo(P.matmul(T.ps4[:, 0:1], T.maskf[:], T.rsum[:, 0:1], True, True))
+    tdo(P.matmul(T.ps4[:, 0:1], T.maskf[:], T.rsum[:, 0:1], True, False))
+    n_c = tdo(P.matmul(T.ps4[:, 0:1], T.maskt[:], T.rsum[:, 1:2], False, True))
     V.wait_ge(S.ts, n_c)
     vwait()
     vdo(V.tensor_scalar(T.i1[:], T.t1[:], T.ps4[:, 0:1], None, A.add))
@@ -213,23 +228,24 @@ def _rank(g, core, T, topo, cores, planes, helpers, rank):
     C.wait_ge(S.l_d, 2 * len(eng))
     C.dma_start(T.win[:, TC:2 * TC], T.x[:]).then_inc(S.s_x, 16)
 
-    W = TC // 4
+    cuts = [0, 128, 448, 768, TC // 2]
     for qu in (V, C):
         qu.wait_ge(S.vs, n_off)
         qu.wait_ge(S.s_x, 16)
-        qu.wait_ge(S.s_r, 2 * M)
-    for k in range(2):
-        a = k * W
-        V.tensor_copy(T.yt[:, a:a + W], T.win[:].indirect(T.off[:, a // 16:(a + W) // 16])).then_inc(S.yv, 1)
-        b = (k + 2) * W
-        C.activation(T.yt[:, b:b + W], T.win[:].indirect(T.off[:, b // 16:(b + W) // 16]), Act.Copy).then_inc(S.ys, 1)
-    for k in range(2):
-        for sem, o in ((S.yv, 0), (S.ys, 2)):
-            a = (k + o) * W
+        qu.wait_ge(S.s_r, 2 * M * (len(eng) * 2 // N))
+    for k in range(len(cuts) - 1):
+        a, z = cuts[k], cuts[k + 1]
+        V.tensor_copy(T.yt[:, a:z], T.win[:].indirect(T.off[:, a // 16:z // 16])).then_inc(S.yv, 1)
+        a, z = a + TC // 2, z + TC // 2
+        C.activation(T.yt[:, a:z], T.win[:].indirect(T.off[:, a // 16:z // 16]), Act.Copy).then_inc(S.ys, 1)
+    for k in range(len(cuts) - 1):
+        for sem, o in ((S.yv, 0), (S.ys, TC // 2)):
+            a, z = cuts[k] + o, cuts[k + 1] + o
             g.sync.wait_ge(sem, k + 1)
-            g.sync.dma_start(T.y[:, a:a + W], T.yt[:, a:a + W]).then_inc(S.s_y, 16)
-    g.sync.wait_ge(S.s_y, 64)
+            g.sync.dma_start(T.y[:, a:z], T.yt[:, a:z]).then_inc(S.s_y, 16)
+    g.sync.wait_ge(S.s_y, 32 * (len(cuts) - 1))
     g.wait_ge(S.l_fl, len(eng))
+    g.wait_ge(S.l_fr, len(eng))
     g.wait_ge(S.l_d, 2 * len(eng))
     g.wait_ge(S.gs, gn[0])
 
@@ -245,12 +261,14 @@ def _helper(g, core, T, topo, cores, planes, helpers, e, i):
     gdo, gwait = _step(g, S.gs, gn)
     tdo, twait = _step(P, S.ts, tn)
 
-    n_mem = vdo(V.memset(T.onef[:, 0:n], 1.0))
-    vdo(V.memset(T.oneb[:], 1.0))
+    vdo(V.memset(T.onef[:, 0:n], 1.0))
+    n_mem = vdo(V.memset(T.oneb[:], 1.0))
     gdo(g.iota(T.pint[:, 0:n], [[0, n]], 0, 1))
     n_iota = gdo(g.iota(T.cint[:, 0:n], [[0, N], [16, w]], 0, 0))
     g.wait_ge(S.vs, n_mem)
-    n_mask = gdo(g.affine_select(T.maskf[:, 0:n], T.onef[:, 0:n], [[16, N], [0, w]], A.is_gt, 0.0, 0, -1))
+    n_mask = gdo(g.affine_select(T.maskf[:, 0:n], T.onef[:, 0:n], [[32, NP], [32 * (1 - e), 2], [0, w]],
+                                 A.is_gt, 0.0, 0, -1))
+    n_mt = gdo(g.affine_select(T.mt[:, 0:n], T.oneb[0:64, 0:n], [[16, NP], [16 * e, 2], [0, w]], A.is_gt, 0.0, 0, -1))
     V.wait_ge(S.gs, n_iota)
     vdo(V.tensor_scalar(T.p15[:, 0:n], T.pint[:, 0:n], 15, None, A.bitwise_and))
     vwait()
@@ -258,29 +276,40 @@ def _helper(g, core, T, topo, cores, planes, helpers, e, i):
     vwait()
     vdo(V.tensor_scalar(T.vc[:, 0:n], T.sint[:, 0:n], -1.0, float(TC - 1 - base), A.mult, A.add))
 
-    dsts = [c for c in helpers[1 - e] if topo.mates(c, core)] + [c for c in cores if topo.mates(c, core)]
-    eng = _engines(topo, core, dsts)
-    per = len(eng) // len(planes[e])
-    g.wait_ge(S.s_fa, 4 * len(eng))
-    tr = []
-    for k, r in enumerate(planes[e]):
-        tr.append(RemoteDMATransfer(
-            dst_ids=[_dst(topo, d, core) for d in dsts], dma_engine_mask=sum(eng[k * per:(k + 1) * per]),
-            remote_sem=S.s_fb, srcs=[T.fland[r]], dsts=[T.fland[r] for d in dsts]))
-    g.remote_dma_fused(tr, local_sem=S.l_rel)
+    there = [c for c in helpers[1 - e] if topo.mates(c, core)]
+    ranks = [c for c in cores if topo.mates(c, core)]
+    eng = _engines(topo, core, there + ranks)
+    per = len(eng) // NP
 
-    g.sync.wait_ge(S.s_fa, 4 * len(eng))
-    g.sync.wait_ge(S.s_fb, len(eng))
-    g.sync.dma_start(T.fall[:], T.fland[:]).then_inc(S.s_fall, 16)
+    def relay(dst, land, lsem):
+        g.remote_dma_fused([RemoteDMATransfer(
+            dst_ids=[_dst(topo, dst, core)], dma_engine_mask=sum(eng[k * per:(k + 1) * per]),
+            remote_sem=S.s_fb, srcs=[T.fown[k]], dsts=[land(k)]) for k in range(NP)], local_sem=lsem)
+    g.wait_ge(S.s_fa, NP * len(eng))
+    relay(there[0], lambda k: T.tfl[:, 16 * k:16 * (k + 1)], S.l_rel)
+    for c in ranks:
+        relay(c, lambda k: T.foth[k], S.l_rr)
+
+    g.sync.wait_ge(S.s_fa, NP * len(eng))
+    g.sync.dma_start(T.ofl[:], T.fown[:]).then_inc(S.s_fall, 16)
     V.wait_ge(S.s_fall, 16)
-    vdo(V.tensor_copy(T.fallf[:], T.fall[:]))
+    vdo(V.tensor_copy(T.oflf[:], T.ofl[:]))
     vwait()
-    vdo(V.tensor_reduce(T.rsum[:, 0:1], T.fallf[:], AxisListType.X, A.add))
+    vdo(V.tensor_reduce(T.rsum[:, 0:1], T.oflf[:], AxisListType.X, A.add))
     vwait()
     V.wait_ge(S.gs, n_mask)
     n_me = vdo(V.tensor_scalar(T.me[:, 0:n], T.maskf[:, 0:n], T.rsum[:, 0:1], None, A.mult))
     P.wait_ge(S.vs, n_me)
-    n_c = tdo(P.matmul(T.ps1[:, 0:n], T.oneb[:], T.me[:, 0:n], True, True))
+    tdo(P.matmul(T.ps1[:, 0:n], T.oneb[:], T.me[:, 0:n], True, False))
+    V.wait_ge(S.s_fb, len(eng))
+    n_tf = vdo(V.tensor_copy(T.tfb[:], T.tfl[:]))
+    P.wait_ge(S.vs, n_tf)
+    n_cs = tdo(P.matmul(T.ps2[0:64, 0:128], T.tfb[:], T.oneb[:], True, True))
+    V.wait_ge(S.ts, n_cs)
+    n_cc = vdo(V.tensor_copy(T.cs[:], T.ps2[0:64, 0:128]))
+    P.wait_ge(S.vs, n_cc)
+    P.wait_ge(S.gs, n_mt)
+    n_c = tdo(P.matmul(T.ps1[:, 0:n], T.cs[:], T.mt[:, 0:n], False, True))
     V.wait_ge(S.ts, n_c)
     vwait()
     vdo(V.tensor_tensor(T.i1[:, 0:n], T.ps1[:, 0:n], T.vc[:, 0:n], A.add))
@@ -292,23 +321,26 @@ def _helper(g, core, T, topo, cores, planes, helpers, e, i):
     vwait()
     n_off = vdo(V.tensor_copy(T.off[:, 0:n], T.i3[:, 0:n]))
 
-    W = N * B // 2
     for qu in (V, C):
         qu.wait_ge(S.vs, n_off)
-        qu.wait_ge(S.s_d, 4 * (len(eng) * 2 // M))
-    V.tensor_copy(T.pick[:, 0:W], T.part[:].indirect(T.off[:, 0:W // 16])).then_inc(S.pv, 1)
-    C.activation(T.pick[:, W:2 * W], T.part[:].indirect(T.off[:, W // 16:n]), Act.Copy).then_inc(S.pa, 1)
-
+        qu.wait_ge(S.s_d, NP * (len(eng) * 2 // M))
     eng2 = _engines(topo, core, cores)
-    per = len(eng2) // N
-    g.wait_ge(S.pv, 1)
-    g.wait_ge(S.pa, 1)
-    tr = []
-    for r in range(N):
-        tr.append(RemoteDMATransfer(
-            dst_ids=[_dst(topo, cores[r], core)], dma_engine_mask=sum(eng2[r * per:(r + 1) * per]), remote_sem=S.s_r,
-            srcs=[T.pick[:, r * B:(r + 1) * B]], dsts=[T.win[:, base:base + B]]))
-    g.remote_dma_fused(tr, local_sem=S.l_s)
+    per2 = len(eng2) * 2 // N
+    for k, a in enumerate((0, 2) if i % 2 == 0 else (2, 0)):
+        b = a + NP
+        V.tensor_copy(T.pick[:, a * B:(a + 2) * B], T.part[:].indirect(T.off[:, a * w:(a + 2) * w])).then_inc(S.pv, 1)
+        C.activation(T.pick[:, b * B:(b + 2) * B], T.part[:].indirect(T.off[:, b * w:(b + 2) * w]),
+                     Act.Copy).then_inc(S.pa, 1)
+        g.wait_ge(S.pv, k + 1)
+        g.wait_ge(S.pa, k + 1)
+        tr = []
+        for m, r in enumerate((a, a + 1, b, b + 1)):
+            tr.append(RemoteDMATransfer(
+                dst_ids=[_dst(topo, cores[r], core)], dma_engine_mask=sum(eng2[m * per2:(m + 1) * per2]),
+                remote_sem=S.s_r, srcs=[T.pick[:, r * B:(r + 1) * B]], dsts=[T.win[:, base:base + B]]))
+        g.remote_dma_fused(tr, local_sem=S.l_s)
     g.wait_ge(S.l_rel, len(eng))
-    g.wait_ge(S.l_s, len(eng2))
+    if ranks:
+        g.wait_ge(S.l_rr, len(eng))
+    g.wait_ge(S.l_s, 2 * len(eng2))
     g.wait_ge(S.gs, gn[0])

@@ -56,7 +56,7 @@ SCRATCH = {
     "yt": ("sbuf", [128, TC], "float32"),
 }
 SEMAPHORES = ["s_fl", "s_f16", "s_st0", "s_st1", "s_x", "s_y", "s_fall", "s_oth", "s_fa", "s_fb", "s_d", "s_r",
-              "l_fl", "l_fr", "l_d", "l_rel", "l_rr", "l_s", "vs", "gs", "ts", "yv", "ys", "pv", "pa"]
+              "l_fl", "l_d", "l_rel", "l_rr", "l_s", "vs", "gs", "ts", "yv", "ys", "pv", "pa"]
 
 _CACHE = {}
 
@@ -72,16 +72,29 @@ def _layout(topo, cores):
     owners = [c for c in range(NCORES) if c not in cores and all(topo.may_write(c, r) for r in cores)]
     helpers = [[], []]
     for e in range(2):
-        for r in planes[e]:
-            k = cores[r]
+        for j in range(NP):
+            k = cores[planes[e][j]]
             helpers[e].append([c for c in owners if topo.host(c) == topo.host(k) and topo.chip(c) == topo.chip(k)
                                and topo.die(c) == topo.die(k)][0])
-    for e in range(2):
-        for r in planes[1 - e]:
-            k = cores[r]
+            k = cores[planes[1 - e][j]]
             helpers[e].append([c for c in owners if topo.mates(c, k) and topo.die(c) != topo.die(k)][0])
     _CACHE["lay"] = (planes, helpers)
     return _CACHE["lay"]
+
+
+def _stage1(j, ne):
+    away = [(2 * j + i) % M for i in range(1, M)]
+    return [[(i, ne // 4) for i in away[:4]], [(i, ne // 2) for i in away[4:6]], [(away[6], ne), (2 * j, 2)]]
+
+
+def _runs(blocks):
+    out = []
+    for i in sorted(blocks):
+        if out and out[-1][1] == i:
+            out[-1][1] = i + 1
+        else:
+            out.append([i, i + 1])
+    return out
 
 
 def _dst(topo, dst, src):
@@ -129,35 +142,39 @@ def _rank(g, core, T, topo, cores, planes, helpers, rank):
     e = rank % 2
     q = planes[e].index(rank)
     V, P, C = g.vector, g.tensor, g.scalar
+    eng = _engines(topo, core, helpers[e])
+    spare = [b for b in _engines(topo, core, [helpers[e][2 * q]]) if b not in eng]
+    calls = _stage1(q, len(eng))
 
     g.sync.dma_start(T.fown[q], T.fl[:]).then_inc(S.s_fl, 16)
-    H = SQ // 2
-    C.dma_start(T.stt[:, 0:H], T.st[:, 0:H]).then_inc(S.s_st0, 16)
-    C.dma_start(T.stt[:, H:SQ], T.st[:, H:SQ]).then_inc(S.s_st1, 16)
+    head = [i for i, _ in calls[0]]
+    n_st = []
+    for sem, blocks in ((S.s_st0, head), (S.s_st1, [i for i in range(M) if i not in head])):
+        for a, z in _runs(blocks):
+            C.dma_start(T.stt[:, a * B:z * B], T.st[:, a * B:z * B]).then_inc(sem, 16)
+        n_st.append(16 * len(_runs(blocks)))
     g.sync.dma_start(T.f16[:], T.fl[:]).then_inc(S.s_f16, 16)
 
-    peers = [cores[r] for r in planes[e] if r != rank]
-    eng = _engines(topo, core, helpers[e] + peers)
-
-    def flags(dsts, lsem):
-        g.remote_dma_fused([RemoteDMATransfer(
-            dst_ids=[_dst(topo, d, core) for d in dsts], dma_engine_mask=sum(eng), remote_sem=S.s_fa,
-            srcs=[T.fown[q]], dsts=[T.fown[q] for d in dsts])], local_sem=lsem)
     g.wait_ge(S.s_fl, 16)
-    flags(helpers[e], S.l_fl)
-    half = M // 2
-    per = len(eng) // half
-    for h in range(2):
-        g.wait_ge(S.s_st0 if h == 0 else S.s_st1, 16)
-        tr = []
-        for k in range(half):
-            i = h * half + k
+    g.remote_dma_fused([RemoteDMATransfer(
+        dst_ids=[_dst(topo, d, core) for d in helpers[e]], dma_engine_mask=sum(eng), remote_sem=S.s_fa,
+        srcs=[T.fown[q]], dsts=[T.fown[q] for d in helpers[e]])], local_sem=S.l_fl)
+    n_ld = 0
+    for h, call in enumerate(calls):
+        if h < 2:
+            g.wait_ge(S.s_st0 if h == 0 else S.s_st1, n_st[h])
+        tr, used = [], 0
+        for i, k in call:
+            if i == 2 * q:
+                m = spare[0:k]
+            else:
+                m = eng[used:used + k]
+                used += k
+            n_ld += k
             tr.append(RemoteDMATransfer(
-                dst_ids=[_dst(topo, helpers[e][i], core)], dma_engine_mask=sum(eng[k * per:(k + 1) * per]),
+                dst_ids=[_dst(topo, helpers[e][i], core)], dma_engine_mask=sum(m),
                 remote_sem=S.s_d, srcs=[T.stt[:, i * B:(i + 1) * B]], dsts=[T.part[:, q * B:(q + 1) * B]]))
         g.remote_dma_fused(tr, local_sem=S.l_d)
-        if h == 0:
-            flags(peers, S.l_fr)
 
     vn, gn, tn = [0], [0], [0]
     vdo, vwait = _step(V, S.vs, vn)
@@ -197,18 +214,19 @@ def _rank(g, core, T, topo, cores, planes, helpers, rank):
     vwait()
     vdo(V.tensor_tensor(T.xc[:], T.vc[:], T.nf[:], A.mult))
 
-    g.sync.wait_ge(S.s_fb, len(eng))
-    g.sync.dma_start(T.tfl[:], T.foth[:]).then_inc(S.s_oth, 16)
+    per = len(eng) // NP
     g.sync.wait_ge(S.s_fl, 16)
-    g.sync.wait_ge(S.s_fa, (NP - 1) * len(eng))
+    g.sync.wait_ge(S.s_fa, (NP - 1) * per)
     g.sync.dma_start(T.ofl[:], T.fown[:]).then_inc(S.s_fall, 16)
-    V.wait_ge(S.s_oth, 16)
-    vdo(V.tensor_copy(T.tflf[:], T.tfl[:]))
+    g.sync.wait_ge(S.s_fb, NP * per)
+    g.sync.dma_start(T.tfl[:], T.foth[:]).then_inc(S.s_oth, 16)
     V.wait_ge(S.s_fall, 16)
     vdo(V.tensor_copy(T.oflf[:], T.ofl[:]))
+    V.wait_ge(S.s_oth, 16)
+    vdo(V.tensor_copy(T.tflf[:], T.tfl[:]))
     vwait()
-    vdo(V.tensor_reduce(T.rsum[:, 1:2], T.tflf[:], AxisListType.X, A.add))
-    n_rs = vdo(V.tensor_reduce(T.rsum[:, 0:1], T.oflf[:], AxisListType.X, A.add))
+    vdo(V.tensor_reduce(T.rsum[:, 0:1], T.oflf[:], AxisListType.X, A.add))
+    n_rs = vdo(V.tensor_reduce(T.rsum[:, 1:2], T.tflf[:], AxisListType.X, A.add))
     P.wait_ge(S.gs, n_mask)
     P.wait_ge(S.vs, n_rs)
     tdo(P.matmul(T.ps4[:, 0:1], T.maskf[:], T.rsum[:, 0:1], True, False))
@@ -225,10 +243,10 @@ def _rank(g, core, T, topo, cores, planes, helpers, rank):
     vwait()
     n_off = vdo(V.tensor_copy(T.off[:], T.i1[:]))
 
-    C.wait_ge(S.l_d, 2 * len(eng))
+    C.wait_ge(S.l_d, n_ld)
     C.dma_start(T.win[:, TC:2 * TC], T.x[:]).then_inc(S.s_x, 16)
 
-    cuts = [0, 128, 448, 768, TC // 2]
+    cuts = [0, 192, 512, 800, TC // 2]
     for qu in (V, C):
         qu.wait_ge(S.vs, n_off)
         qu.wait_ge(S.s_x, 16)
@@ -245,8 +263,7 @@ def _rank(g, core, T, topo, cores, planes, helpers, rank):
             g.sync.dma_start(T.y[:, a:z], T.yt[:, a:z]).then_inc(S.s_y, 16)
     g.sync.wait_ge(S.s_y, 32 * (len(cuts) - 1))
     g.wait_ge(S.l_fl, len(eng))
-    g.wait_ge(S.l_fr, len(eng))
-    g.wait_ge(S.l_d, 2 * len(eng))
+    g.wait_ge(S.l_d, n_ld)
     g.wait_ge(S.gs, gn[0])
 
 
@@ -276,19 +293,24 @@ def _helper(g, core, T, topo, cores, planes, helpers, e, i):
     vwait()
     vdo(V.tensor_scalar(T.vc[:, 0:n], T.sint[:, 0:n], -1.0, float(TC - 1 - base), A.mult, A.add))
 
-    there = [c for c in helpers[1 - e] if topo.mates(c, core)]
-    ranks = [c for c in cores if topo.mates(c, core)]
-    eng = _engines(topo, core, there + ranks)
+    there = [c for c in helpers[1 - e] if topo.mates(c, core)][0]
+    away = [c for c in cores if topo.mates(c, core)]
+    here = [r for r in planes[e] if topo.host(cores[r]) == topo.host(core) and topo.chip(cores[r]) == topo.chip(core)]
+    eng = _engines(topo, core, [there])
     per = len(eng) // NP
 
-    def relay(dst, land, lsem):
+    def relay(dst, slots, land, rsem, lsem):
         g.remote_dma_fused([RemoteDMATransfer(
             dst_ids=[_dst(topo, dst, core)], dma_engine_mask=sum(eng[k * per:(k + 1) * per]),
-            remote_sem=S.s_fb, srcs=[T.fown[k]], dsts=[land(k)]) for k in range(NP)], local_sem=lsem)
+            remote_sem=rsem, srcs=[T.fown[k]], dsts=[land(k)]) for k in slots], local_sem=lsem)
+        return len(slots) * per
+    every = list(range(NP))
     g.wait_ge(S.s_fa, NP * len(eng))
-    relay(there[0], lambda k: T.tfl[:, 16 * k:16 * (k + 1)], S.l_rel)
-    for c in ranks:
-        relay(c, lambda k: T.foth[k], S.l_rr)
+    relay(there, every, lambda k: T.tfl[:, 16 * k:16 * (k + 1)], S.s_fb, S.l_rel)
+    if away:
+        n_rr = relay(away[0], every, lambda k: T.foth[k], S.s_fb, S.l_rr)
+    else:
+        n_rr = relay(cores[here[0]], [k for k in every if planes[e][k] != here[0]], lambda k: T.fown[k], S.s_fa, S.l_rr)
 
     g.sync.wait_ge(S.s_fa, NP * len(eng))
     g.sync.dma_start(T.ofl[:], T.fown[:]).then_inc(S.s_fall, 16)
@@ -301,7 +323,7 @@ def _helper(g, core, T, topo, cores, planes, helpers, e, i):
     n_me = vdo(V.tensor_scalar(T.me[:, 0:n], T.maskf[:, 0:n], T.rsum[:, 0:1], None, A.mult))
     P.wait_ge(S.vs, n_me)
     tdo(P.matmul(T.ps1[:, 0:n], T.oneb[:], T.me[:, 0:n], True, False))
-    V.wait_ge(S.s_fb, len(eng))
+    V.wait_ge(S.s_fb, NP * per)
     n_tf = vdo(V.tensor_copy(T.tfb[:], T.tfl[:]))
     P.wait_ge(S.vs, n_tf)
     n_cs = tdo(P.matmul(T.ps2[0:64, 0:128], T.tfb[:], T.oneb[:], True, True))
@@ -321,12 +343,13 @@ def _helper(g, core, T, topo, cores, planes, helpers, e, i):
     vwait()
     n_off = vdo(V.tensor_copy(T.off[:, 0:n], T.i3[:, 0:n]))
 
+    n_d = sum(k for j in range(NP) for call in _stage1(j, len(eng)) for h, k in call if h == i)
     for qu in (V, C):
         qu.wait_ge(S.vs, n_off)
-        qu.wait_ge(S.s_d, NP * (len(eng) * 2 // M))
+        qu.wait_ge(S.s_d, n_d)
     eng2 = _engines(topo, core, cores)
     per2 = len(eng2) * 2 // N
-    for k, a in enumerate((0, 2) if i % 2 == 0 else (2, 0)):
+    for k, a in enumerate((0, 2) if i // 2 % 2 == 0 else (2, 0)):
         b = a + NP
         V.tensor_copy(T.pick[:, a * B:(a + 2) * B], T.part[:].indirect(T.off[:, a * w:(a + 2) * w])).then_inc(S.pv, 1)
         C.activation(T.pick[:, b * B:(b + 2) * B], T.part[:].indirect(T.off[:, b * w:(b + 2) * w]),
@@ -339,8 +362,7 @@ def _helper(g, core, T, topo, cores, planes, helpers, e, i):
                 dst_ids=[_dst(topo, cores[r], core)], dma_engine_mask=sum(eng2[m * per2:(m + 1) * per2]),
                 remote_sem=S.s_r, srcs=[T.pick[:, r * B:(r + 1) * B]], dsts=[T.win[:, base:base + B]]))
         g.remote_dma_fused(tr, local_sem=S.l_s)
-    g.wait_ge(S.l_rel, len(eng))
-    if ranks:
-        g.wait_ge(S.l_rr, len(eng))
+    g.wait_ge(S.l_rel, NP * per)
+    g.wait_ge(S.l_rr, n_rr)
     g.wait_ge(S.l_s, 2 * len(eng2))
     g.wait_ge(S.gs, gn[0])

from concourse.bass import DstId, RemoteDMATransfer
from concourse.mybir import AluOpType as A, AxisListType, ActivationFunctionType as Act

N = 8
NP = N // 2
TC = 2048
SQ = 1024
M = 8
B = SQ // M
NCORES = 256

SCRATCH = {
    "fown": ("dram", [NP, 128, 16], "int32"),
    "foth": ("dram", [NP, 128, 16], "int32"),
    "ofl": ("sbuf", [128, 64], "int32"),
    "tfl": ("sbuf", [128, 64], "int32"),
    "oflf": ("sbuf", [128, 64], "float32"),
    "tflf": ("sbuf", [128, 64], "float32"),
    "rsum": ("sbuf", [128, 8], "float32"),
    "pint": ("sbuf", [128, 128], "int32"),
    "cint": ("sbuf", [128, 128], "int32"),
    "p15": ("sbuf", [128, 128], "int32"),
    "sint": ("sbuf", [128, 128], "int32"),
    "vc": ("sbuf", [128, 128], "float32"),
    "onef": ("sbuf", [128, 128], "float32"),
    "maskf": ("sbuf", [128, 128], "float32"),
    "maskt": ("sbuf", [128, 128], "float32"),
    "i1": ("sbuf", [128, 128], "int32"),
    "i2": ("sbuf", [128, 128], "int32"),
    "i3": ("sbuf", [128, 128], "int32"),
    "off": ("sbuf", [128, 128], "uint16"),
    "ps1": ("psum", [128, 512], "float32"),
    "ps2": ("psum", [128, 512], "float32"),
    "ps3": ("psum", [128, 512], "float32"),
    "ps4": ("psum", [128, 512], "float32"),
    "oneb": ("sbuf", [128, 128], "bfloat16"),
    "me": ("sbuf", [128, 64], "bfloat16"),
    "tfb": ("sbuf", [128, 64], "bfloat16"),
    "cs": ("sbuf", [64, 128], "bfloat16"),
    "mt": ("sbuf", [64, 64], "bfloat16"),
    "part": ("sbuf", [128, NP * B], "float32"),
    "pick": ("sbuf", [128, N * B], "float32"),
    "f16": ("sbuf", [16, 128], "int32"),
    "fb": ("sbuf", [16, 128], "bfloat16"),
    "zb": ("sbuf", [16, 128], "bfloat16"),
    "leq": ("sbuf", [16, 128], "bfloat16"),
    "lpre": ("sbuf", [16, 128], "bfloat16"),
    "zero": ("sbuf", [128, 128], "float32"),
    "cum": ("sbuf", [128, 128], "float32"),
    "t1": ("sbuf", [128, 128], "float32"),
    "nf": ("sbuf", [128, 128], "float32"),
    "fr": ("sbuf", [128, 128], "float32"),
    "xc": ("sbuf", [128, 128], "float32"),
    "stt": ("sbuf", [128, SQ], "float32"),
    "win": ("sbuf", [128, 2 * TC], "float32"),
    "yt": ("sbuf", [128, TC], "float32"),
}
SEMAPHORES = ["s_fl", "s_f16", "s_st0", "s_st1", "s_x", "s_y", "s_fall", "s_oth", "s_fa", "s_fb", "s_d", "s_r",
              "l_fl", "l_d", "l_rel", "l_rr", "l_s", "vs", "gs", "ts", "yv", "ys", "pv", "pa"]

_CACHE = {}


def _layout(topo, cores):
    if "lay" in _CACHE:
        return _CACHE["lay"]
    first = [r for r in range(N) if r == 0 or topo.same_plane(cores[0], cores[r])]
    planes = [first, [r for r in range(N) if r not in first]]
    for e in range(2):
        if planes[e] != list(range(e, N, 2)):
            raise ValueError("the design needs the stream's even parts in one plane, the odd ones in the other")
    owners = [c for c in range(NCORES) if c not in cores and all(topo.may_write(c, r) for r in cores)]
    helpers = [[], []]
    for e in range(2):
        for j in range(NP):
            k = cores[planes[e][j]]
            helpers[e].append([c for c in owners if topo.host(c) == topo.host(k) and topo.chip(c) == topo.chip(k)
                               and topo.die(c) == topo.die(k)][0])
            k = cores[planes[1 - e][j]]
            helpers[e].append([c for c in owners if topo.mates(c, k) and topo.die(c) != topo.die(k)][0])
    _CACHE["lay"] = (planes, helpers)
    return _CACHE["lay"]


def _stage1(j, ne):
    away = [(2 * j + i) % M for i in range(1, M)]
    return [[(i, ne // 4) for i in away[:4]], [(i, ne // 2) for i in away[4:6]], [(away[6], ne), (2 * j, 2)]]


def _runs(blocks):
    out = []
    for i in sorted(blocks):
        if out and out[-1][1] == i:
            out[-1][1] = i + 1
        else:
            out.append([i, i + 1])
    return out


def _dst(topo, dst, src):
    rid, pid = topo.addr(dst, src)
    return DstId(rid=rid, pnc=pid)


def _engines(topo, src, dsts):
    m = topo.mask(src, dsts[0])
    for d in dsts[1:]:
        m &= topo.mask(src, d)
    out, b = [], 1
    while b <= m:
        if m & b:
            out.append(b)
        b *= 2
    return out


def _step(q, sem, n):
    def do(ins):
        ins.then_inc(sem, 1)
        n[0] += 1
        return n[0]

    def wait():
        q.wait_ge(sem, n[0])
    return do, wait


def rank_program(g, core, T, topo):
    cores = list(T.cores)
    planes, helpers = _layout(topo, cores)
    rank = T.rank_of(core)
    if rank is not None:
        _rank(g, core, T, topo, cores, planes, helpers, rank)
        return
    for e in range(2):
        if core in helpers[e]:
            _helper(g, core, T, topo, cores, planes, helpers, e, helpers[e].index(core))


def _rank(g, core, T, topo, cores, planes, helpers, rank):
    S = T.sem
    e = rank % 2
    q = planes[e].index(rank)
    V, P, C = g.vector, g.tensor, g.scalar
    eng = _engines(topo, core, helpers[e])
    spare = [b for b in _engines(topo, core, [helpers[e][2 * q]]) if b not in eng]
    calls = _stage1(q, len(eng))

    g.sync.dma_start(T.fown[q], T.fl[:]).then_inc(S.s_fl, 16)
    head = [i for i, _ in calls[0]]
    n_st = []
    for sem, blocks in ((S.s_st0, head), (S.s_st1, [i for i in range(M) if i not in head])):
        for a, z in _runs(blocks):
            C.dma_start(T.stt[:, a * B:z * B], T.st[:, a * B:z * B]).then_inc(sem, 16)
        n_st.append(16 * len(_runs(blocks)))
    g.sync.dma_start(T.f16[:], T.fl[:]).then_inc(S.s_f16, 16)

    g.wait_ge(S.s_fl, 16)
    g.remote_dma_fused([RemoteDMATransfer(
        dst_ids=[_dst(topo, d, core) for d in helpers[e]], dma_engine_mask=sum(eng), remote_sem=S.s_fa,
        srcs=[T.fown[q]], dsts=[T.fown[q] for d in helpers[e]])], local_sem=S.l_fl)
    n_ld = 0
    for h, call in enumerate(calls):
        if h < 2:
            g.wait_ge(S.s_st0 if h == 0 else S.s_st1, n_st[h])
        tr, used = [], 0
        for i, k in call:
            if i == 2 * q:
                m = spare[0:k]
            else:
                m = eng[used:used + k]
                used += k
            n_ld += k
            tr.append(RemoteDMATransfer(
                dst_ids=[_dst(topo, helpers[e][i], core)], dma_engine_mask=sum(m),
                remote_sem=S.s_d, srcs=[T.stt[:, i * B:(i + 1) * B]], dsts=[T.part[:, q * B:(q + 1) * B]]))
        g.remote_dma_fused(tr, local_sem=S.l_d)

    vn, gn, tn = [0], [0], [0]
    vdo, vwait = _step(V, S.vs, vn)
    gdo, gwait = _step(g, S.gs, gn)
    tdo, twait = _step(P, S.ts, tn)
    vdo(V.memset(T.oneb[0:16, :], 1.0))
    vdo(V.memset(T.zb[:], 0.0))
    vdo(V.memset(T.zero[:], 0.0))
    n_mem = vdo(V.memset(T.onef[:], 1.0))
    g.wait_ge(S.vs, n_mem)
    gdo(g.affine_select(T.lpre[:], T.zb[:], [[0, 8], [1, 16]], A.is_gt, -1.0, 0, -1))
    n_lhs = gdo(g.affine_select(T.leq[:], T.oneb[0:16, :], [[0, 8], [1, 16]], A.is_equal, 0.0, 0, -1))
    gdo(g.iota(T.pint[:], [[0, 128]], 0, 1))
    n_iota = gdo(g.iota(T.cint[:], [[16, 128]], TC, 0))
    gdo(g.affine_select(T.maskf[:], T.onef[:], [[0, 128]], A.is_gt, 0.0, 32 * q, -1))
    n_mask = gdo(g.affine_select(T.maskt[:], T.onef[:], [[0, 128]], A.is_gt, 0.0, 32 * (q + e), -1))

    V.wait_ge(S.s_f16, 16)
    n_fb = vdo(V.tensor_copy(T.fb[:], T.f16[:]))
    P.wait_ge(S.vs, n_fb)
    n_a = tdo(P.matmul(T.ps1[:, 0:128], T.oneb[0:16, :], T.fb[:], True, True))
    P.wait_ge(S.gs, n_lhs)
    tdo(P.matmul(T.ps2[:, 0:128], T.lpre[:], T.fb[:], True, True))
    n_e = tdo(P.matmul(T.ps3[:, 0:128], T.leq[:], T.fb[:], True, True))
    V.wait_ge(S.ts, n_a)
    V.wait_ge(S.vs, n_fb)
    vdo(V.tensor_tensor_scan(T.cum[:], T.ps1[:, 0:128], T.zero[:], 0.0, A.add, A.add))
    V.wait_ge(S.ts, n_e)
    vwait()
    vdo(V.tensor_tensor(T.t1[:], T.cum[:], T.ps2[:, 0:128], A.add))
    vdo(V.tensor_copy(T.fr[:], T.ps3[:, 0:128]))
    vdo(V.tensor_scalar(T.nf[:], T.ps3[:, 0:128], -1.0, 1.0, A.mult, A.add))
    V.wait_ge(S.gs, n_iota)
    vdo(V.tensor_scalar(T.p15[:], T.pint[:], 15, None, A.bitwise_and))
    vwait()
    vdo(V.tensor_tensor(T.vc[:], T.p15[:], T.cint[:], A.add))
    vwait()
    vdo(V.tensor_tensor(T.xc[:], T.vc[:], T.nf[:], A.mult))

    per = len(eng) // NP
    g.sync.wait_ge(S.s_fl, 16)
    g.sync.wait_ge(S.s_fa, (NP - 1) * per)
    g.sync.dma_start(T.ofl[:], T.fown[:]).then_inc(S.s_fall, 16)
    g.sync.wait_ge(S.s_fb, NP * per)
    g.sync.dma_start(T.tfl[:], T.foth[:]).then_inc(S.s_oth, 16)
    V.wait_ge(S.s_fall, 16)
    vdo(V.tensor_copy(T.oflf[:], T.ofl[:]))
    V.wait_ge(S.s_oth, 16)
    vdo(V.tensor_copy(T.tflf[:], T.tfl[:]))
    vwait()
    vdo(V.tensor_reduce(T.rsum[:, 0:1], T.oflf[:], AxisListType.X, A.add))
    n_rs = vdo(V.tensor_reduce(T.rsum[:, 1:2], T.tflf[:], AxisListType.X, A.add))
    P.wait_ge(S.gs, n_mask)
    P.wait_ge(S.vs, n_rs)
    tdo(P.matmul(T.ps4[:, 0:1], T.maskf[:], T.rsum[:, 0:1], True, False))
    n_c = tdo(P.matmul(T.ps4[:, 0:1], T.maskt[:], T.rsum[:, 1:2], False, True))
    V.wait_ge(S.ts, n_c)
    vwait()
    vdo(V.tensor_scalar(T.i1[:], T.t1[:], T.ps4[:, 0:1], None, A.add))
    vwait()
    vdo(V.tensor_scalar(T.i2[:], T.i1[:], TC - 1, None, A.bitwise_and))
    vwait()
    vdo(V.tensor_tensor(T.i3[:], T.i2[:], T.fr[:], A.mult))
    vwait()
    vdo(V.tensor_tensor(T.i1[:], T.i3[:], T.xc[:], A.add))
    vwait()
    n_off = vdo(V.tensor_copy(T.off[:], T.i1[:]))

    C.wait_ge(S.l_d, n_ld)
    C.dma_start(T.win[:, TC:2 * TC], T.x[:]).then_inc(S.s_x, 16)

    cuts = [0, 192, 512, 800, TC // 2]
    for qu in (V, C):
        qu.wait_ge(S.vs, n_off)
        qu.wait_ge(S.s_x, 16)
        qu.wait_ge(S.s_r, 2 * M * (len(eng) * 2 // N))
    for k in range(len(cuts) - 1):
        a, z = cuts[k], cuts[k + 1]
        V.tensor_copy(T.yt[:, a:z], T.win[:].indirect(T.off[:, a // 16:z // 16])).then_inc(S.yv, 1)
        a, z = a + TC // 2, z + TC // 2
        C.activation(T.yt[:, a:z], T.win[:].indirect(T.off[:, a // 16:z // 16]), Act.Copy).then_inc(S.ys, 1)
    for k in range(len(cuts) - 1):
        for sem, o in ((S.yv, 0), (S.ys, TC // 2)):
            a, z = cuts[k] + o, cuts[k + 1] + o
            g.sync.wait_ge(sem, k + 1)
            g.sync.dma_start(T.y[:, a:z], T.yt[:, a:z]).then_inc(S.s_y, 16)
    g.sync.wait_ge(S.s_y, 32 * (len(cuts) - 1))
    g.wait_ge(S.l_fl, len(eng))
    g.wait_ge(S.l_d, n_ld)
    g.wait_ge(S.gs, gn[0])


def _helper(g, core, T, topo, cores, planes, helpers, e, i):
    S = T.sem
    V, P, C = g.vector, g.tensor, g.scalar
    base = e * SQ + i * B
    n = N * B // 16
    w = B // 16
    vn, gn, tn = [0], [0], [0]
    vdo, vwait = _step(V, S.vs, vn)
    gdo, gwait = _step(g, S.gs, gn)
    tdo, twait = _step(P, S.ts, tn)

    vdo(V.memset(T.onef[:, 0:n], 1.0))
    n_mem = vdo(V.memset(T.oneb[:], 1.0))
    gdo(g.iota(T.pint[:, 0:n], [[0, n]], 0, 1))
    n_iota = gdo(g.iota(T.cint[:, 0:n], [[0, N], [16, w]], 0, 0))
    g.wait_ge(S.vs, n_mem)
    n_mask = gdo(g.affine_select(T.maskf[:, 0:n], T.onef[:, 0:n], [[32, NP], [32 * (1 - e), 2], [0, w]],
                                 A.is_gt, 0.0, 0, -1))
    n_mt = gdo(g.affine_select(T.mt[:, 0:n], T.oneb[0:64, 0:n], [[16, NP], [16 * e, 2], [0, w]], A.is_gt, 0.0, 0, -1))
    V.wait_ge(S.gs, n_iota)
    vdo(V.tensor_scalar(T.p15[:, 0:n], T.pint[:, 0:n], 15, None, A.bitwise_and))
    vwait()
    vdo(V.tensor_tensor(T.sint[:, 0:n], T.p15[:, 0:n], T.cint[:, 0:n], A.add))
    vwait()
    vdo(V.tensor_scalar(T.vc[:, 0:n], T.sint[:, 0:n], -1.0, float(TC - 1 - base), A.mult, A.add))

    there = [c for c in helpers[1 - e] if topo.mates(c, core)][0]
    away = [c for c in cores if topo.mates(c, core)]
    here = [r for r in planes[e] if topo.host(cores[r]) == topo.host(core) and topo.chip(cores[r]) == topo.chip(core)]
    eng = _engines(topo, core, [there])
    per = len(eng) // NP

    def relay(dst, slots, land, rsem, lsem):
        g.remote_dma_fused([RemoteDMATransfer(
            dst_ids=[_dst(topo, dst, core)], dma_engine_mask=sum(eng[k * per:(k + 1) * per]),
            remote_sem=rsem, srcs=[T.fown[k]], dsts=[land(k)]) for k in slots], local_sem=lsem)
        return len(slots) * per
    every = list(range(NP))
    g.wait_ge(S.s_fa, NP * len(eng))
    relay(there, every, lambda k: T.tfl[:, 16 * k:16 * (k + 1)], S.s_fb, S.l_rel)
    if away:
        n_rr = relay(away[0], every, lambda k: T.foth[k], S.s_fb, S.l_rr)
    else:
        n_rr = relay(cores[here[0]], [k for k in every if planes[e][k] != here[0]], lambda k: T.fown[k], S.s_fa, S.l_rr)

    g.sync.wait_ge(S.s_fa, NP * len(eng))
    g.sync.dma_start(T.ofl[:], T.fown[:]).then_inc(S.s_fall, 16)
    V.wait_ge(S.s_fall, 16)
    vdo(V.tensor_copy(T.oflf[:], T.ofl[:]))
    vwait()
    vdo(V.tensor_reduce(T.rsum[:, 0:1], T.oflf[:], AxisListType.X, A.add))
    vwait()
    V.wait_ge(S.gs, n_mask)
    n_me = vdo(V.tensor_scalar(T.me[:, 0:n], T.maskf[:, 0:n], T.rsum[:, 0:1], None, A.mult))
    P.wait_ge(S.vs, n_me)
    tdo(P.matmul(T.ps1[:, 0:n], T.oneb[:], T.me[:, 0:n], True, False))
    V.wait_ge(S.s_fb, NP * per)
    n_tf = vdo(V.tensor_copy(T.tfb[:], T.tfl[:]))
    P.wait_ge(S.vs, n_tf)
    n_cs = tdo(P.matmul(T.ps2[0:64, 0:128], T.tfb[:], T.oneb[:], True, True))
    V.wait_ge(S.ts, n_cs)
    n_cc = vdo(V.tensor_copy(T.cs[:], T.ps2[0:64, 0:128]))
    P.wait_ge(S.vs, n_cc)
    P.wait_ge(S.gs, n_mt)
    n_c = tdo(P.matmul(T.ps1[:, 0:n], T.cs[:], T.mt[:, 0:n], False, True))
    V.wait_ge(S.ts, n_c)
    vwait()
    vdo(V.tensor_tensor(T.i1[:, 0:n], T.ps1[:, 0:n], T.vc[:, 0:n], A.add))
    vwait()
    sh = (TC // B).bit_length() - 1
    vdo(V.tensor_scalar(T.i2[:, 0:n], T.i1[:, 0:n], sh, 3 * B, A.arith_shift_right, A.bitwise_and))
    vwait()
    vdo(V.tensor_tensor(T.i3[:, 0:n], T.i2[:, 0:n], T.sint[:, 0:n], A.add))
    vwait()
    n_off = vdo(V.tensor_copy(T.off[:, 0:n], T.i3[:, 0:n]))

    n_d = sum(k for j in range(NP) for call in _stage1(j, len(eng)) for h, k in call if h == i)
    for qu in (V, C):
        qu.wait_ge(S.vs, n_off)
        qu.wait_ge(S.s_d, n_d)
    eng2 = _engines(topo, core, cores)
    per2 = len(eng2) * 2 // N
    for k, a in enumerate((0, 2) if i // 2 % 2 == 0 else (2, 0)):
        b = a + NP
        V.tensor_copy(T.pick[:, a * B:(a + 2) * B], T.part[:].indirect(T.off[:, a * w:(a + 2) * w])).then_inc(S.pv, 1)
        C.activation(T.pick[:, b * B:(b + 2) * B], T.part[:].indirect(T.off[:, b * w:(b + 2) * w]),
                     Act.Copy).then_inc(S.pa, 1)
        g.wait_ge(S.pv, k + 1)
        g.wait_ge(S.pa, k + 1)
        tr = []
        for m, r in enumerate((a, a + 1, b, b + 1)):
            tr.append(RemoteDMATransfer(
                dst_ids=[_dst(topo, cores[r], core)], dma_engine_mask=sum(eng2[m * per2:(m + 1) * per2]),
                remote_sem=S.s_r, srcs=[T.pick[:, r * B:(r + 1) * B]], dsts=[T.win[:, base:base + B]]))
        g.remote_dma_fused(tr, local_sem=S.l_s)
    g.wait_ge(S.l_rel, NP * per)
    g.wait_ge(S.l_rr, n_rr)
    g.wait_ge(S.l_s, 2 * len(eng2))
    g.wait_ge(S.gs, gn[0])
